import numpy as np
import ml_dtypes


def mxq(x, axis, fmt="e4m3"):
    dtype, down = {"e4m3": (ml_dtypes.float8_e4m3fn, 7), "e5m2": (ml_dtypes.float8_e5m2, 14)}[fmt]
    v = np.moveaxis(np.asarray(x, np.float32).astype(ml_dtypes.bfloat16).astype(np.float64), axis, -1)
    blocks = v.reshape(v.shape[:-1] + (-1, 32))
    amax = np.abs(blocks).max(-1, keepdims=True)
    byte = np.maximum(np.where(amax > 0, np.frexp(amax)[1] - 1 + 127, 0) - down, 1)
    scale = np.exp2(byte - 127.0)
    codes = (blocks / scale).astype(np.float32).astype(dtype).astype(np.float64)
    return np.moveaxis((codes * scale).reshape(v.shape), -1, axis)


WIDE = False


def mx_kscale(k):
    if not WIDE:
        return np.ones(k)
    levels = np.array([10, -10, 5, -5, 0])
    if k % 512:
        return np.exp2(np.random.permutation(np.resize(levels, k // 32))).repeat(32)
    a = np.empty((k // 512, 16))
    for p in range(k // 512):
        a[p, :8] = np.random.permutation(np.resize(levels, 8))
        for g in range(8):
            far = levels[np.abs(levels - a[p, g]) >= 10]
            a[p, g + 8] = far[np.random.randint(len(far))]
    return np.exp2(a.ravel()).repeat(32)


def f64(x):
    return np.asarray(x).astype(np.float64)


def striped(idx):
    return np.tile(idx.reshape(-1, 16).T, (8, 1)).astype(np.uint16)


def unstriped(offs):
    return offs[:16].T.reshape(-1).astype(np.int64)


def striped8(idx):
    return np.concatenate([x.reshape(-1, 16).T for x in idx]).astype(np.uint16)


def runs(offs, k):
    lists = np.stack([offs[16 * r : 16 * r + 16].T.reshape(-1) for r in range(8)]).astype(np.int64)
    return lists[np.arange(k) % 512 // 64]


def pack_weight(w):
    k, n = w.shape
    w = f64(np.asarray(w, np.float32).astype(ml_dtypes.bfloat16)).reshape(k // 32, 32, n)
    amax = np.abs(w).max(1)
    byte = np.clip(np.where(amax > 0, np.frexp(amax)[1] - 1 + 127 - 7, 1), 1, 254)
    scaled = (w * np.exp2(127.0 - byte)[:, None, :]).reshape(k, n).astype(np.float32)
    words = np.ascontiguousarray(scaled.reshape(k // 512, 128, 4, n).transpose(0, 1, 3, 2)).astype(ml_dtypes.float8_e4m3fn).view(np.uint8)
    return words, np.ascontiguousarray(byte.astype(np.uint8).reshape(k // 512, 16, n))


def unpack_weight(words, scales):
    g, p, n, _ = words.shape
    vals = np.ascontiguousarray(words).view(ml_dtypes.float8_e4m3fn).astype(np.float64) * np.repeat(np.exp2(scales.astype(np.float64) - 127.0), 8, axis=1)[..., None]
    return vals.transpose(0, 1, 3, 2).reshape(g * 512, n)

def planes(y):
    n, m = y.shape
    v = y.astype(np.float32).astype(ml_dtypes.bfloat16).astype(np.float64).reshape(n // 32, 32, m)
    top = np.abs(v).max(1)
    byte = np.clip(np.where(top > 0, np.frexp(top)[1] - 1 + 127 - 7, 1), 1, 254)
    codes = (v * np.exp2(127.0 - byte)[:, None, :]).reshape(n, m).astype(np.float32).astype(ml_dtypes.float8_e4m3fn).view(np.uint8)
    words = codes.reshape(n // 512, 128, 4, m).transpose(0, 1, 3, 2)
    return np.ascontiguousarray(words), np.ascontiguousarray(byte.astype(np.uint8).reshape(n // 512, 16, m))


K, T, S, V, N = 512, 2048, 512, 512, 512
P = 2 ** 7


def setup_inputs():
    n = np.random.standard_normal
    s = mx_kscale(K)[:, None]
    packed_xT = pack_weight(n((K, T)) * s)
    return {
        "x_words": packed_xT[0],
        "x_scales": packed_xT[1],
        "w1": (n((K, N)) / np.sqrt(K) / s).astype(np.float32),
        "w2": (n((K, N)) / np.sqrt(K) / s).astype(np.float32),
        "pi1": np.tile(np.random.uniform(0.2, 0.8, S), (P, 1)).astype(np.float32),
        "pi2": np.tile(np.random.uniform(0.2, 0.8, S), (P, 1)).astype(np.float32),
        "offs": striped(np.random.permutation(T)[:S]),
        "cen": striped(np.random.permutation(T)[:V]),
        "k1": striped8(np.random.randint(0, V, (8, S))),
        "k2": striped8(np.random.randint(0, V, (8, S))),
    }


def reference(x_words, x_scales, w1, w2, pi1, pi2, offs, cen, k1, k2):
    xq = unpack_weight(x_words, x_scales)[:, unstriped(offs)]
    y = mxq(f64(w1), 0, "e4m3").T @ xq
    x_cen = unpack_weight(x_words, x_scales)[:, unstriped(cen)]
    c = mxq(f64(w2), 0, "e4m3").T @ x_cen
    out_0 = np.log(f64(pi1)[:1] * (np.exp(-0.125 * ((y - (c[np.arange(N)[:, None], runs(k1, N)])) ** 2))) + f64(pi2)[:1] * (np.exp(-0.125 * ((y - (c[np.arange(N)[:, None], runs(k2, N)])) ** 2))))
    return (out_0,) + planes(out_0)

@@ -1,0 +1,331 @@
+import math
+from contextlib import ExitStack
+
+import concourse.mybir as mybir
+from concourse.masks import make_identity
+
+K, T, S, V, N = 512, 2048, 512, 512, 512
+FLOPS = 2 * K * N * (S + V)
+
+F32 = mybir.dt.float32
+BF16 = mybir.dt.bfloat16
+I32 = mybir.dt.int32
+U32 = mybir.dt.uint32
+U16 = mybir.dt.uint16
+U8 = mybir.dt.uint8
+FP8X4 = mybir.dt.float8_e4m3fn_x4
+ACT = mybir.ActivationFunctionType
+ALU = mybir.AluOpType
+
+P = 128
+PACK = 4
+CHUNK = 128
+CHUNKS = S // CHUNK
+LIST_COLS = CHUNK // 16
+HALF = N // 2
+SLOT = 4 * N
+CAST_S = (1, 1, 1, 0)
+CCOPY_S = (1, 1, 1, 1)
+ABS_S = (1, 1, 0, 0)
+ROUND_S = (1, 1, 0, 0)
+RES_S = (0, 0, 0, 0)
+QSPLIT = 2
+HOLD_WORDS = 2
+W1_HALVES = 0
+W2_HALVES = 1
+SPLIT_LAST = 0
+WIDE0 = 0
+ORDER = "c p x s o a b 1 k"
+V_ON_G = 0
+YBANKS = 4
+YEARLY = 4
+GAP_ORDER = "a0 a1 m0 m1 a2 m2 a3 m3"
+GS = (0, 1, 2, 0)
+
+
+def tile_picked_gmm8_none_po_kernel(
+    tc, x_words, x_scales, w1, w2, pi1, pi2, offs, cen, k1, k2, out_0, out_1, out_2
+):
+    nc = tc.nc
+    with ExitStack() as ctx:
+        keep = ctx.enter_context(tc.tile_pool(name="keep", bufs=1))
+        reuse = ctx.enter_context(tc.tile_pool(name="reuse", bufs=1))
+        work = ctx.enter_context(tc.tile_pool(name="work", bufs=1))
+        held = ctx.enter_context(tc.tile_pool(name="held", bufs=1))
+        late = ctx.enter_context(tc.tile_pool(name="late", bufs=1))
+        psum = ctx.enter_context(tc.psum_pool(name="psum", bufs=1))
+
+        def slot(tag, name):
+            return work.tile([P, PACK, CHUNK], F32, name=name, tag=tag)
+
+        def placed(name, offset, width=CHUNK):
+            return held.tile([P, PACK, width], F32, name=name, offset=offset)
+
+        def bank(tag, name):
+            return psum.tile([P, PACK, CHUNK], F32, name=name, tag=tag)
+
+        def flat(tile):
+            return tile[:].rearrange("p t j -> p (t j)")
+
+        xs = keep.tile([P, T], U8, name="xs", align_bytes=64)
+        nc.vector.memset(xs[:].bitcast(I32), 0)
+        ident = keep.tile([P, P], F32, name="ident")
+        make_identity(nc, ident[:])
+
+        cen_sb = keep.tile([P, V // 16], U16, name="cen_sb")
+        offs_sb = keep.tile([P, S // 16], U16, name="offs_sb")
+        k_sb = [keep.tile([P, S // 16], U16, name=f"k{i + 1}_sb") for i in range(2)]
+        pi_col = [keep.tile([P, CHUNKS], F32, name=f"pi{i + 1}_col") for i in range(2)]
+        xw = keep.tile([P, T], I32, name="xw", align_bytes=64)
+        if W2_HALVES:
+            w2_raw = [keep.tile([P, PACK, HALF], F32, name=f"w2_raw{h}") for h in range(2)]
+        else:
+            w2_whole = keep.tile([P, PACK, N], F32, name="w2_whole")
+            w2_raw = [w2_whole[:, :, HALF * h : HALF * (h + 1)] for h in range(2)]
+        if W1_HALVES:
+            w1_raw = [keep.tile([P, PACK, HALF], F32, name=f"w1_raw{h}") for h in range(2)]
+        else:
+            w1_whole = keep.tile([P, PACK, N], F32, name="w1_whole")
+            w1_raw = [w1_whole[:, :, HALF * h : HALF * (h + 1)] for h in range(2)]
+
+        def half(w, h):
+            return w.rearrange("(p j) m -> p j m", j=PACK)[:, :, HALF * h : HALF * (h + 1)]
+
+        for what in ORDER.split():
+            if what == "c":
+                nc.sync.dma_start(cen_sb[:], cen)
+            if what == "o":
+                nc.sync.dma_start(offs_sb[:], offs)
+            if what == "k":
+                nc.sync.dma_start(k_sb[0][:], k1)
+                nc.sync.dma_start(k_sb[1][:], k2)
+            if what == "p":
+                for i, pi in enumerate((pi1, pi2)):
+                    with nc.allow_non_contiguous_dma(reason="one weight a partition and chunk"):
+                        nc.scalar.dma_start(pi_col[i][:], pi[0:1, :].rearrange("o (b q) -> q (o b)", b=CHUNKS))
+            if what == "x":
+                nc.sync.dma_start(xw[:], x_words[0].rearrange("p n t -> p (n t)").bitcast(I32))
+            if what == "s":
+                for q in range(4):
+                    nc.sync.dma_start(
+                        xs[32 * q : 32 * q + 4, :].bitcast(I32), x_scales[0, 4 * q : 4 * q + 4, :].bitcast(I32)
+                    )
+            if what == "a" and not W2_HALVES:
+                nc.sync.dma_start(w2_whole[:], w2.rearrange("(p j) m -> p j m", j=PACK))
+            if what == "a" and W2_HALVES:
+                nc.sync.dma_start(w2_raw[0][:], half(w2, 0))
+            if what == "b" and W2_HALVES:
+                nc.sync.dma_start(w2_raw[1][:], half(w2, 1))
+            if what == "1":
+                if W1_HALVES:
+                    for h in range(2):
+                        nc.sync.dma_start(w1_raw[h][:], half(w1, h))
+                else:
+                    nc.sync.dma_start(w1_whole[:], w1.rearrange("(p j) m -> p j m", j=PACK))
+
+        log_pi = keep.tile([P, 2 * CHUNKS], F32, name="log_pi")
+        for i in range(2):
+            nc.scalar.activation(log_pi[:, CHUNKS * i : CHUNKS * (i + 1)], pi_col[i][:], ACT.Ln)
+        warm = keep.tile([P, 2], F32, name="warm")
+        nc.scalar.activation(warm[:], log_pi[:, CHUNKS - 1 : CHUNKS + 1], ACT.Tanh)
+        log_ratio = keep.tile([P, CHUNKS], F32, name="log_ratio")
+        nc.gpsimd.tensor_tensor(log_ratio[:], log_pi[:, 0:CHUNKS], log_pi[:, CHUNKS : 2 * CHUNKS], ALU.subtract)
+        inv_pi2 = keep.tile([P, CHUNKS], F32, name="inv_pi2")
+        nc.vector.reciprocal(inv_pi2[:], pi_col[0][:])
+        half_inv = keep.tile([P, CHUNKS], F32, name="half_inv")
+        nc.gpsimd.tensor_scalar(half_inv[:], inv_pi2[:], 0.5, 0.0, ALU.mult, ALU.add)
+        tanh_bias = late.tile([P, CHUNKS], F32, name="tanh_bias", offset=0)
+        nc.gpsimd.tensor_scalar(tanh_bias[:], log_ratio[:], -0.5, 0.0, ALU.mult, ALU.add)
+
+        def gather_columns(lst, words, scales):
+            nc.vector.tensor_copy(words[:], xw[:].bitcast(U32).indirect(lst[:]))
+            nc.vector.tensor_copy(scales[:], xs[:].indirect(lst[:]))
+
+        def round_half(raw, grouped, h, on_scalar):
+            dst = grouped[:, :, 64 * h : 64 * (h + 1), :].rearrange("p t m j -> p m t j")
+            src = raw[:].rearrange("p j (m t) -> p m t j", t=PACK)
+            if on_scalar:
+                nc.scalar.copy(dst, src)
+            else:
+                nc.vector.tensor_copy(dst, src)
+
+        def quantise_weight(grouped, name):
+            codes = keep.tile([P, PACK, P], U32, name=f"{name}_codes", align_bytes=64)
+            scales = keep.tile([P, PACK, P], U8, name=f"{name}_scales", align_bytes=64)
+            step = PACK // QSPLIT
+            for t in range(0, PACK, step):
+                nc.vector.quantize_mx(
+                    out=codes[:, t : t + step, :].rearrange("p t m -> p (t m)").bitcast(FP8X4),
+                    scales=scales[:, t : t + step, :].rearrange("p t m -> p (t m)"),
+                    in_=grouped[:, t : t + step, :, :].rearrange("p t m j -> p (t m j)"),
+                )
+            return codes, scales
+
+        xc_words = keep.tile([P, V], U32, name="xc_words", align_bytes=64)
+        xc_scales = keep.tile([P, V], U8, name="xc_scales", align_bytes=64)
+        gather_columns(cen_sb, xc_words, xc_scales)
+        w2_grouped = reuse.tile([P, PACK, P, PACK], BF16, name="w2_grouped", align_bytes=64, offset=0)
+        round_half(w2_raw[0], w2_grouped, 0, CAST_S[0])
+        round_half(w2_raw[1], w2_grouped, 1, CAST_S[1])
+        w2_codes, w2_scales = quantise_weight(w2_grouped, "w2")
+        w1_grouped = keep.tile([P, PACK, P, PACK], BF16, name="w1_grouped", align_bytes=64)
+        if CAST_S[2]:
+            round_half(w1_raw[0], w1_grouped, 0, True)
+        if CAST_S[3] == 1:
+            round_half(w1_raw[1], w1_grouped, 1, True)
+        neg_c = []
+        for t in range(PACK):
+            c_bank = bank(f"a{t}", f"c_bank{t}")
+            nc.tensor.matmul_mx(
+                out=flat(c_bank),
+                lhsT=w2_codes[:, t, :].bitcast(FP8X4),
+                lhsT_scale=w2_scales[:, t, :],
+                rhs=xc_words[:].bitcast(FP8X4),
+                rhs_scale=xc_scales[:],
+                start=True,
+                stop=True,
+            )
+            window = keep.tile([P, V], F32, name=f"neg_c{t}")
+            if CCOPY_S[t]:
+                nc.scalar.activation(window[:], flat(c_bank), ACT.Copy, scale=-1.0)
+            else:
+                nc.vector.tensor_scalar(window[:], flat(c_bank), -1.0, None, ALU.mult)
+            neg_c.append(window)
+
+        xo_words = reuse.tile([P, S], U32, name="xo_words", align_bytes=64, offset=0 if HOLD_WORDS == 1 else 8 * S)
+        xo_scales = reuse.tile([P, S], U8, name="xo_scales", align_bytes=64, offset=4 * S if HOLD_WORDS < 2 else 12 * S)
+        gather_columns(offs_sb, xo_words, xo_scales)
+        if not CAST_S[2]:
+            round_half(w1_raw[0], w1_grouped, 0, False)
+        if CAST_S[3] != 1:
+            round_half(w1_raw[1], w1_grouped, 1, CAST_S[3] == 2)
+        w1_codes, w1_scales = quantise_weight(w1_grouped, "w1")
+        y_banks = []
+
+        def project(b):
+            y_bank = bank(f"d{b % YBANKS}", f"y_bank{b}")
+            cols = slice(CHUNK * b, CHUNK * (b + 1))
+            for t in range(PACK):
+                nc.tensor.matmul_mx(
+                    out=y_bank[:, t, :],
+                    lhsT=w1_codes[:, t, :].bitcast(FP8X4),
+                    lhsT_scale=w1_scales[:, t, :],
+                    rhs=xo_words[:, cols].bitcast(FP8X4),
+                    rhs_scale=xo_scales[:, cols],
+                    start=True,
+                    stop=True,
+                )
+            y_banks.append(y_bank)
+
+        for b in range(YEARLY):
+            project(b)
+        q2_all = keep.tile([P, CHUNKS, N], F32, name="q2_all")
+        v_all = keep.tile([P, CHUNKS, N], F32, name="v_all")
+        th_all = keep.tile([P, CHUNKS, N], F32, name="th_all")
+        q1, sg, gap = {}, {}, []
+
+        def distances(b):
+            if b >= YEARLY:
+                project(b)
+            y = slot(f"y{b}", f"y{b}")
+            nc.scalar.copy(flat(y), flat(y_banks[b]))
+            for i in range(2):
+                if b < 2:
+                    g = slot(f"g{GS[2 * b + i]}", f"g{i}_{b}")
+                else:
+                    g = placed(f"g{i}_{b}", 2 * SLOT * (b - 2) + SLOT * i)
+                d_bank = bank(f"a{(2 * b + i) % 4}", f"d_bank{i}_{b}")
+                for t in range(PACK):
+                    nc.tensor.matmul(d_bank[:, t, :], y[:, t, :], ident[:], start=(t == 0), stop=False, is_transpose=True)
+                for t in range(PACK):
+                    nc.vector.tensor_copy(
+                        g[:, t, :], neg_c[t][:].indirect(k_sb[i][:, LIST_COLS * b : LIST_COLS * (b + 1)])
+                    )
+                    nc.tensor.matmul(
+                        d_bank[:, t, :], g[:, t, :], ident[:], start=False, stop=(t == PACK - 1), is_transpose=True
+                    )
+                if i == 0:
+                    q1[b] = placed(f"q1_{b}", 2 * SLOT * b + SLOT // 2)
+                    dst = flat(q1[b])
+                else:
+                    dst = q2_all[:, b, :]
+                nc.scalar.activation(dst, flat(d_bank), ACT.Square, scale=math.sqrt(0.125))
+
+        def exponentials(b):
+            (nc.gpsimd if b < V_ON_G else nc.vector).tensor_tensor(v_all[:, b, :], flat(q1[b]), q2_all[:, b, :], ALU.subtract)
+            nc.scalar.activation(th_all[:, b, :], v_all[:, b, :], ACT.Tanh, scale=0.5, bias=tanh_bias[:, b : b + 1])
+            if ABS_S[b]:
+                magnitude(b)
+
+        def magnitude(b):
+            if ABS_S[b]:
+                sg[b] = flat(slot(f"sg{b}", f"sg{b}"))
+                nc.scalar.activation(sg[b], th_all[:, b, :], ACT.Abs)
+            else:
+                sg[b] = gap[0][:, CHUNKS + b, :]
+                nc.vector.scalar_tensor_tensor(sg[b], th_all[:, b, :], -1.0, th_all[:, b, :], ALU.mult, ALU.max)
+
+        for b in range(CHUNKS):
+            if b >= 2:
+                exponentials(b - 2)
+            distances(b)
+        exponentials(CHUNKS - 2)
+        exponentials(CHUNKS - 1)
+
+        out_banks = {}
+        gap.append(held.tile([P, 2 * CHUNKS, N], F32, name="gap", offset=2 * SLOT * (CHUNKS - 1) + SLOT // 2))
+        for step in GAP_ORDER.split():
+            b = int(step[1])
+            if step[0] == "a":
+                if not ABS_S[b]:
+                    magnitude(b)
+                continue
+            mn = gap[0][:, b, :]
+            nc.vector.scalar_tensor_tensor(
+                mn, v_all[:, b, :], log_ratio[:, b : b + 1], q2_all[:, b, :], ALU.min, ALU.add
+            )
+            out_banks[b] = bank(f"d{b}", f"out_bank{b}")
+            for t in range(PACK):
+                nc.tensor.matmul(
+                    out_banks[b][:, t, :], mn[:, P * t : P * (t + 1)], ident[:],
+                    start=(t == 0), stop=False, is_transpose=True,
+                )
+
+        lg_all = late.tile([P, CHUNKS, N], F32, name="lg_all", offset=0)
+        words = keep.tile([P, S], U32, name="words", align_bytes=64)
+        scales = keep.tile([P, S], U8, name="scales", align_bytes=64)
+        out_rows = out_0.rearrange("(p t) j -> p t j", t=PACK)
+        out_words = out_1[0].rearrange("p n t -> p (n t)").bitcast(I32)
+        for b in range(CHUNKS):
+            cols = slice(CHUNK * b, CHUNK * (b + 1))
+            lg = lg_all[:, b, :]
+            nc.scalar.activation(lg, sg[b], ACT.Ln, scale=half_inv[:, b : b + 1], bias=half_inv[:, b : b + 1])
+            for t in range(PACK):
+                nc.tensor.matmul(
+                    out_banks[b][:, t, :], lg[:, P * t : P * (t + 1)], ident[:], start=False, stop=(t == PACK - 1), is_transpose=True
+                )
+            res = slot(f"res{b}", f"res{b}")
+            if RES_S[b]:
+                nc.scalar.activation(flat(res), flat(out_banks[b]), ACT.Copy, scale=-1.0)
+            else:
+                nc.vector.tensor_scalar(flat(res), flat(out_banks[b]), -1.0, None, ALU.mult)
+            nc.sync.dma_start(out_rows[:, :, cols], res[:])
+            rounded = work.tile([P, CHUNK, PACK], BF16, name=f"rounded{b}", align_bytes=64)
+            if ROUND_S[b]:
+                nc.scalar.copy(rounded[:], res[:].rearrange("p t j -> p j t"))
+            else:
+                nc.vector.tensor_copy(rounded[:], res[:].rearrange("p t j -> p j t"))
+            nc.vector.quantize_mx(
+                out=words[:, cols].bitcast(FP8X4),
+                scales=scales[:, cols],
+                in_=rounded[:].rearrange("p j t -> p (j t)"),
+            )
+            if b == CHUNKS - 2:
+                nc.scalar.dma_start(out_words[:, 0 : CHUNK * (b + 1)], words[:, 0 : CHUNK * (b + 1)].bitcast(I32))
+            if b == CHUNKS - 1:
+                nc.sync.dma_start(out_words[:, cols], words[:, cols].bitcast(I32))
+        for q in range(4):
+            queue = nc.scalar if q % 2 == 0 else nc.sync
+            queue.dma_start(
+                out_2[0, 4 * q : 4 * q + 4, :].bitcast(I32), scales[32 * q : 32 * q + 4, :].bitcast(I32)
+            )

@@ -27,19 +27,22 @@ SLOT = 4 * N
 CAST_S = (1, 1, 1, 0)
 CCOPY_S = (1, 1, 1, 1)
 ABS_S = (1, 1, 0, 0)
-ROUND_S = (1, 1, 0, 0)
-RES_S = (0, 0, 0, 0)
+ROUND_S = (0, 0, 0, 0)
+RES_S = (0, 0, 1, 1)
 QSPLIT = 2
 HOLD_WORDS = 2
 W1_HALVES = 0
 W2_HALVES = 1
 SPLIT_LAST = 0
 WIDE0 = 0
-ORDER = "c p x s o a b 1 k"
+ORDER = "c p o x s a b 1 k"
 V_ON_G = 0
 YBANKS = 4
 YEARLY = 4
-GAP_ORDER = "a0 a1 m0 m1 a2 m2 a3 m3"
+CLOCKS = 0
+W1_SHARES = 1
+PLAN = "g020_s0 g021_x g220_s0 v0 g211_q00 v1 g311_q10 v2 v3"
+GAP_ORDER = "a0 a1 m0 m1 m2 m3 a2 a3"
 GS = (0, 1, 2, 0)
 
 
@@ -67,6 +70,8 @@ def tile_picked_gmm8_none_po_kernel(
         def flat(tile):
             return tile[:].rearrange("p t j -> p (t j)")
 
+        pi_rows = keep.tile([P, P], F32, name="pi_rows")
+        nc.gpsimd.memset(pi_rows[:], 0.0)
         xs = keep.tile([P, T], U8, name="xs", align_bytes=64)
         nc.vector.memset(xs[:].bitcast(I32), 0)
         ident = keep.tile([P, P], F32, name="ident")
@@ -75,7 +80,6 @@ def tile_picked_gmm8_none_po_kernel(
         cen_sb = keep.tile([P, V // 16], U16, name="cen_sb")
         offs_sb = keep.tile([P, S // 16], U16, name="offs_sb")
         k_sb = [keep.tile([P, S // 16], U16, name=f"k{i + 1}_sb") for i in range(2)]
-        pi_col = [keep.tile([P, CHUNKS], F32, name=f"pi{i + 1}_col") for i in range(2)]
         xw = keep.tile([P, T], I32, name="xw", align_bytes=64)
         if W2_HALVES:
             w2_raw = [keep.tile([P, PACK, HALF], F32, name=f"w2_raw{h}") for h in range(2)]
@@ -101,8 +105,9 @@ def tile_picked_gmm8_none_po_kernel(
                 nc.sync.dma_start(k_sb[1][:], k2)
             if what == "p":
                 for i, pi in enumerate((pi1, pi2)):
-                    with nc.allow_non_contiguous_dma(reason="one weight a partition and chunk"):
-                        nc.scalar.dma_start(pi_col[i][:], pi[0:1, :].rearrange("o (b q) -> q (o b)", b=CHUNKS))
+                    nc.scalar.dma_start(
+                        pi_rows[CHUNKS * i : CHUNKS * (i + 1), :], pi[0:1, :].rearrange("o (b q) -> (o b) q", b=CHUNKS)
+                    )
             if what == "x":
                 nc.sync.dma_start(xw[:], x_words[0].rearrange("p n t -> p (n t)").bitcast(I32))
             if what == "s":
@@ -123,17 +128,14 @@ def tile_picked_gmm8_none_po_kernel(
                 else:
                     nc.sync.dma_start(w1_whole[:], w1.rearrange("(p j) m -> p j m", j=PACK))
 
-        log_pi = keep.tile([P, 2 * CHUNKS], F32, name="log_pi")
-        for i in range(2):
-            nc.scalar.activation(log_pi[:, CHUNKS * i : CHUNKS * (i + 1)], pi_col[i][:], ACT.Ln)
-        warm = keep.tile([P, 2], F32, name="warm")
-        nc.scalar.activation(warm[:], log_pi[:, CHUNKS - 1 : CHUNKS + 1], ACT.Tanh)
+        pi_bank = bank("d0", "pi_bank")
+        nc.tensor.transpose(pi_bank[:, 0, :], pi_rows[:], ident[:])
+        log_pi = reuse.tile([P, 2 * CHUNKS], F32, name="log_pi", align_bytes=64, offset=0)
+        nc.scalar.activation(log_pi[:], pi_bank[:, 0, 0 : 2 * CHUNKS], ACT.Ln)
+        half_inv = keep.tile([P, CHUNKS], F32, name="half_inv")
+        nc.scalar.activation(half_inv[:], log_pi[:, 0:CHUNKS], ACT.Exp, scale=-1.0, bias=math.log(0.5))
         log_ratio = keep.tile([P, CHUNKS], F32, name="log_ratio")
         nc.gpsimd.tensor_tensor(log_ratio[:], log_pi[:, 0:CHUNKS], log_pi[:, CHUNKS : 2 * CHUNKS], ALU.subtract)
-        inv_pi2 = keep.tile([P, CHUNKS], F32, name="inv_pi2")
-        nc.vector.reciprocal(inv_pi2[:], pi_col[0][:])
-        half_inv = keep.tile([P, CHUNKS], F32, name="half_inv")
-        nc.gpsimd.tensor_scalar(half_inv[:], inv_pi2[:], 0.5, 0.0, ALU.mult, ALU.add)
         tanh_bias = late.tile([P, CHUNKS], F32, name="tanh_bias", offset=0)
         nc.gpsimd.tensor_scalar(tanh_bias[:], log_ratio[:], -0.5, 0.0, ALU.mult, ALU.add)
 
@@ -167,8 +169,11 @@ def tile_picked_gmm8_none_po_kernel(
         w2_grouped = reuse.tile([P, PACK, P, PACK], BF16, name="w2_grouped", align_bytes=64, offset=0)
         round_half(w2_raw[0], w2_grouped, 0, CAST_S[0])
         round_half(w2_raw[1], w2_grouped, 1, CAST_S[1])
+        if CLOCKS:
+            clock = keep.tile([P, 2], F32, name="clock")
+            nc.gpsimd.tensor_copy(clock[:, 1:2], w2_grouped[:, 3, 127, 0:1])
         w2_codes, w2_scales = quantise_weight(w2_grouped, "w2")
-        w1_grouped = keep.tile([P, PACK, P, PACK], BF16, name="w1_grouped", align_bytes=64)
+        w1_grouped = reuse.tile([P, PACK, P, PACK], BF16, name="w1_grouped", align_bytes=64, offset=0 if W1_SHARES else 16 * S)
         if CAST_S[2]:
             round_half(w1_raw[0], w1_grouped, 0, True)
         if CAST_S[3] == 1:
@@ -193,7 +198,7 @@ def tile_picked_gmm8_none_po_kernel(
             neg_c.append(window)
 
         xo_words = reuse.tile([P, S], U32, name="xo_words", align_bytes=64, offset=0 if HOLD_WORDS == 1 else 8 * S)
-        xo_scales = reuse.tile([P, S], U8, name="xo_scales", align_bytes=64, offset=4 * S if HOLD_WORDS < 2 else 12 * S)
+        xo_scales = reuse.tile([P, S], U8, name="xo_scales", align_bytes=64, offset=12 * S)
         gather_columns(offs_sb, xo_words, xo_scales)
         if not CAST_S[2]:
             round_half(w1_raw[0], w1_grouped, 0, False)
@@ -224,32 +229,48 @@ def tile_picked_gmm8_none_po_kernel(
         th_all = keep.tile([P, CHUNKS, N], F32, name="th_all")
         q1, sg, gap = {}, {}, []
 
-        def distances(b):
-            if b >= YEARLY:
-                project(b)
-            y = slot(f"y{b}", f"y{b}")
-            nc.scalar.copy(flat(y), flat(y_banks[b]))
-            for i in range(2):
-                if b < 2:
-                    g = slot(f"g{GS[2 * b + i]}", f"g{i}_{b}")
-                else:
-                    g = placed(f"g{i}_{b}", 2 * SLOT * (b - 2) + SLOT * i)
-                d_bank = bank(f"a{(2 * b + i) % 4}", f"d_bank{i}_{b}")
+        ys = {}
+
+        def y_copy(b):
+            ys[b] = slot(f"y{b}", f"y{b}")
+            nc.scalar.copy(flat(ys[b]), flat(y_banks[b]))
+
+        def distances(b0, n, i, hold):
+            name = f"g{i}_{b0}"
+            if hold == "x":
+                g = reuse.tile([P, PACK, n * CHUNK], F32, name=name, align_bytes=64, offset=8 * S)
+            elif hold[0] == "s":
+                g = work.tile([P, PACK, n * CHUNK], F32, name=name, tag=hold)
+            else:
+                g = placed(name, 2 * SLOT * int(hold[1]) + SLOT * int(hold[2]), n * CHUNK)
+            d_banks = []
+            for b in range(b0, b0 + n):
+                if b not in ys:
+                    y_copy(b)
+                d_bank = bank(f"a{count[0] % 4}", f"d_bank{i}_{b}")
+                count.insert(0, count[0] + 1)
                 for t in range(PACK):
-                    nc.tensor.matmul(d_bank[:, t, :], y[:, t, :], ident[:], start=(t == 0), stop=False, is_transpose=True)
-                for t in range(PACK):
-                    nc.vector.tensor_copy(
-                        g[:, t, :], neg_c[t][:].indirect(k_sb[i][:, LIST_COLS * b : LIST_COLS * (b + 1)])
-                    )
+                    nc.tensor.matmul(d_bank[:, t, :], ys[b][:, t, :], ident[:], start=(t == 0), stop=False, is_transpose=True)
+                d_banks.append(d_bank)
+            for t in range(PACK):
+                nc.vector.tensor_copy(
+                    g[:, t, :], neg_c[t][:].indirect(k_sb[i][:, LIST_COLS * b0 : LIST_COLS * (b0 + n)])
+                )
+                for u in range(n):
                     nc.tensor.matmul(
-                        d_bank[:, t, :], g[:, t, :], ident[:], start=False, stop=(t == PACK - 1), is_transpose=True
+                        d_banks[u][:, t, :], g[:, t, CHUNK * u : CHUNK * (u + 1)], ident[:],
+                        start=False, stop=(t == PACK - 1), is_transpose=True,
                     )
+            for u in range(n):
+                b = b0 + u
                 if i == 0:
                     q1[b] = placed(f"q1_{b}", 2 * SLOT * b + SLOT // 2)
                     dst = flat(q1[b])
                 else:
                     dst = q2_all[:, b, :]
-                nc.scalar.activation(dst, flat(d_bank), ACT.Square, scale=math.sqrt(0.125))
+                nc.scalar.activation(dst, flat(d_banks[u]), ACT.Square, scale=math.sqrt(0.125))
+
+        count = [0]
 
         def exponentials(b):
             (nc.gpsimd if b < V_ON_G else nc.vector).tensor_tensor(v_all[:, b, :], flat(q1[b]), q2_all[:, b, :], ALU.subtract)
@@ -265,12 +286,11 @@ def tile_picked_gmm8_none_po_kernel(
                 sg[b] = gap[0][:, CHUNKS + b, :]
                 nc.vector.scalar_tensor_tensor(sg[b], th_all[:, b, :], -1.0, th_all[:, b, :], ALU.mult, ALU.max)
 
-        for b in range(CHUNKS):
-            if b >= 2:
-                exponentials(b - 2)
-            distances(b)
-        exponentials(CHUNKS - 2)
-        exponentials(CHUNKS - 1)
+        for step in PLAN.split():
+            if step[0] == "v":
+                exponentials(int(step[1]))
+            else:
+                distances(int(step[1]), int(step[2]), int(step[3]), step[5:])
 
         out_banks = {}
         gap.append(held.tile([P, 2 * CHUNKS, N], F32, name="gap", offset=2 * SLOT * (CHUNKS - 1) + SLOT // 2))

@@ -27,7 +27,7 @@ SLOT = 4 * N
 CAST_S = (1, 1, 1, 0)
 CCOPY_S = (1, 1, 1, 1)
 ABS_S = (1, 1, 0, 0)
-ROUND_S = (0, 0, 0, 0)
+ROUND_S = (1, 1, 0, 0)
 RES_S = (0, 0, 1, 1)
 QSPLIT = 2
 HOLD_WORDS = 2
@@ -39,10 +39,13 @@ ORDER = "c p o x s a b 1 k"
 V_ON_G = 0
 YBANKS = 4
 YEARLY = 4
+OUT_ORDER = "r0 r1 r2 r3 b0 b1 b2 b3 q0 q1 q2 q3"
+WARM = 1
+W1_SPLIT = 40
 CLOCKS = 0
 W1_SHARES = 1
-PLAN = "g020_s0 g021_x g220_s0 v0 g211_q00 v1 g311_q10 v2 v3"
-GAP_ORDER = "a0 a1 m0 m1 m2 m3 a2 a3"
+PLAN = "g020_s0 g021_x g220_s0 v0 g211_q00 v1 g311_q10 m0_00 v2 v3"
+GAP_ORDER = "a0 a1 m1 a2 a3 n2 n3"
 GS = (0, 1, 2, 0)
 
 
@@ -130,14 +133,15 @@ def tile_picked_gmm8_none_po_kernel(
 
         pi_bank = bank("d0", "pi_bank")
         nc.tensor.transpose(pi_bank[:, 0, :], pi_rows[:], ident[:])
-        log_pi = reuse.tile([P, 2 * CHUNKS], F32, name="log_pi", align_bytes=64, offset=0)
-        nc.scalar.activation(log_pi[:], pi_bank[:, 0, 0 : 2 * CHUNKS], ACT.Ln)
-        half_inv = keep.tile([P, CHUNKS], F32, name="half_inv")
-        nc.scalar.activation(half_inv[:], log_pi[:, 0:CHUNKS], ACT.Exp, scale=-1.0, bias=math.log(0.5))
-        log_ratio = keep.tile([P, CHUNKS], F32, name="log_ratio")
-        nc.gpsimd.tensor_tensor(log_ratio[:], log_pi[:, 0:CHUNKS], log_pi[:, CHUNKS : 2 * CHUNKS], ALU.subtract)
+        log_pi = keep.tile([P, 2 * CHUNKS], F32, name="log_pi")
+        nc.scalar.activation(log_pi[:], pi_bank[:, 0, 0 : 2 * CHUNKS], ACT.Ln, scale=2.0)
+        limit = keep.tile([P, CHUNKS], F32, name="limit")
+        nc.scalar.activation(limit[:], log_pi[:, CHUNKS : 2 * CHUNKS], ACT.Copy, scale=-1.0)
         tanh_bias = late.tile([P, CHUNKS], F32, name="tanh_bias", offset=0)
-        nc.gpsimd.tensor_scalar(tanh_bias[:], log_ratio[:], -0.5, 0.0, ALU.mult, ALU.add)
+        nc.scalar.activation(tanh_bias[:], log_pi[:, CHUNKS : 2 * CHUNKS], ACT.Copy, scale=0.5)
+        if WARM:
+            warm = reuse.tile([P, 1], F32, name="warm", align_bytes=64, offset=0)
+            nc.scalar.activation(warm[:], log_pi[:, 0:1], ACT.Tanh)
 
         def gather_columns(lst, words, scales):
             nc.vector.tensor_copy(words[:], xw[:].bitcast(U32).indirect(lst[:]))
@@ -146,6 +150,14 @@ def tile_picked_gmm8_none_po_kernel(
         def round_half(raw, grouped, h, on_scalar):
             dst = grouped[:, :, 64 * h : 64 * (h + 1), :].rearrange("p t m j -> p m t j")
             src = raw[:].rearrange("p j (m t) -> p m t j", t=PACK)
+            if on_scalar:
+                nc.scalar.copy(dst, src)
+            else:
+                nc.vector.tensor_copy(dst, src)
+
+        def round_part(lo, hi, grouped, on_scalar):
+            dst = grouped[:, :, lo:hi, :].rearrange("p t m j -> p m t j")
+            src = w1_whole[:, :, PACK * lo : PACK * hi].rearrange("p j (m t) -> p m t j", t=PACK)
             if on_scalar:
                 nc.scalar.copy(dst, src)
             else:
@@ -175,7 +187,7 @@ def tile_picked_gmm8_none_po_kernel(
         w2_codes, w2_scales = quantise_weight(w2_grouped, "w2")
         w1_grouped = reuse.tile([P, PACK, P, PACK], BF16, name="w1_grouped", align_bytes=64, offset=0 if W1_SHARES else 16 * S)
         if CAST_S[2]:
-            round_half(w1_raw[0], w1_grouped, 0, True)
+            round_part(0, W1_SPLIT, w1_grouped, True)
         if CAST_S[3] == 1:
             round_half(w1_raw[1], w1_grouped, 1, True)
         neg_c = []
@@ -203,7 +215,7 @@ def tile_picked_gmm8_none_po_kernel(
         if not CAST_S[2]:
             round_half(w1_raw[0], w1_grouped, 0, False)
         if CAST_S[3] != 1:
-            round_half(w1_raw[1], w1_grouped, 1, CAST_S[3] == 2)
+            round_part(W1_SPLIT, P, w1_grouped, False)
         w1_codes, w1_scales = quantise_weight(w1_grouped, "w1")
         y_banks = []
 
@@ -226,16 +238,17 @@ def tile_picked_gmm8_none_po_kernel(
             project(b)
         q2_all = keep.tile([P, CHUNKS, N], F32, name="q2_all")
         v_all = keep.tile([P, CHUNKS, N], F32, name="v_all")
-        th_all = keep.tile([P, CHUNKS, N], F32, name="th_all")
-        q1, sg, gap = {}, {}, []
+        th_all = late.tile([P, CHUNKS, N], F32, name="th_all", offset=CHUNKS * SLOT)
+        q1, sg, gap, out_banks, tanh_banks = {}, {}, [], {}, {}
 
         ys = {}
+        y_pairs = [keep.tile([P, PACK, 2 * CHUNK], F32, name=f"y{h}") for h in range(2)]
 
         def y_copy(b):
-            ys[b] = slot(f"y{b}", f"y{b}")
-            nc.scalar.copy(flat(ys[b]), flat(y_banks[b]))
+            ys[b] = y_pairs[b // 2][:, :, CHUNK * (b % 2) : CHUNK * (b % 2 + 1)]
+            nc.scalar.copy(ys[b], y_banks[b][:])
 
-        def distances(b0, n, i, hold):
+        def distances(b0, n, i, hold, fused):
             name = f"g{i}_{b0}"
             if hold == "x":
                 g = reuse.tile([P, PACK, n * CHUNK], F32, name=name, align_bytes=64, offset=8 * S)
@@ -249,17 +262,20 @@ def tile_picked_gmm8_none_po_kernel(
                     y_copy(b)
                 d_bank = bank(f"a{count[0] % 4}", f"d_bank{i}_{b}")
                 count.insert(0, count[0] + 1)
-                for t in range(PACK):
+                for t in range(0 if fused else PACK):
                     nc.tensor.matmul(d_bank[:, t, :], ys[b][:, t, :], ident[:], start=(t == 0), stop=False, is_transpose=True)
                 d_banks.append(d_bank)
             for t in range(PACK):
-                nc.vector.tensor_copy(
-                    g[:, t, :], neg_c[t][:].indirect(k_sb[i][:, LIST_COLS * b0 : LIST_COLS * (b0 + n)])
-                )
+                looked_up = neg_c[t][:].indirect(k_sb[i][:, LIST_COLS * b0 : LIST_COLS * (b0 + n)])
+                if fused:
+                    first = CHUNK * (b0 % 2)
+                    nc.vector.tensor_tensor(g[:, t, :], looked_up, y_pairs[b0 // 2][:, t, first : first + n * CHUNK], ALU.add)
+                else:
+                    nc.vector.tensor_copy(g[:, t, :], looked_up)
                 for u in range(n):
                     nc.tensor.matmul(
                         d_banks[u][:, t, :], g[:, t, CHUNK * u : CHUNK * (u + 1)], ident[:],
-                        start=False, stop=(t == PACK - 1), is_transpose=True,
+                        start=(fused and t == 0), stop=(t == PACK - 1), is_transpose=True,
                     )
             for u in range(n):
                 b = b0 + u
@@ -273,7 +289,9 @@ def tile_picked_gmm8_none_po_kernel(
         count = [0]
 
         def exponentials(b):
-            (nc.gpsimd if b < V_ON_G else nc.vector).tensor_tensor(v_all[:, b, :], flat(q1[b]), q2_all[:, b, :], ALU.subtract)
+            nc.vector.scalar_tensor_tensor(
+                v_all[:, b, :], flat(q1[b]), log_pi[:, b : b + 1], q2_all[:, b, :], ALU.subtract, ALU.subtract
+            )
             nc.scalar.activation(th_all[:, b, :], v_all[:, b, :], ACT.Tanh, scale=0.5, bias=tanh_bias[:, b : b + 1])
             if ABS_S[b]:
                 magnitude(b)
@@ -286,30 +304,35 @@ def tile_picked_gmm8_none_po_kernel(
                 sg[b] = gap[0][:, CHUNKS + b, :]
                 nc.vector.scalar_tensor_tensor(sg[b], th_all[:, b, :], -1.0, th_all[:, b, :], ALU.mult, ALU.max)
 
+        def turn(src, tag, name):
+            dst = bank(tag, name)
+            for t in range(PACK):
+                nc.tensor.transpose(dst[:, t, :], src[:, P * t : P * (t + 1)], ident[:])
+            return dst
+
+        def minimum(b, mn):
+            nc.vector.scalar_tensor_tensor(mn, v_all[:, b, :], limit[:, b : b + 1], q2_all[:, b, :], ALU.min, ALU.add)
+            out_banks[b] = turn(mn, f"d{b}", f"min_bank{b}")
+
         for step in PLAN.split():
             if step[0] == "v":
                 exponentials(int(step[1]))
+            elif step[0] == "m":
+                minimum(int(step[1]), flat(placed(step, 2 * SLOT * int(step[3]) + SLOT * int(step[4]))))
             else:
-                distances(int(step[1]), int(step[2]), int(step[3]), step[5:])
+                distances(int(step[1]), int(step[2]), int(step[3]), step[5:], step[0] == "f")
 
-        out_banks = {}
         gap.append(held.tile([P, 2 * CHUNKS, N], F32, name="gap", offset=2 * SLOT * (CHUNKS - 1) + SLOT // 2))
         for step in GAP_ORDER.split():
             b = int(step[1])
             if step[0] == "a":
                 if not ABS_S[b]:
                     magnitude(b)
-                continue
-            mn = gap[0][:, b, :]
-            nc.vector.scalar_tensor_tensor(
-                mn, v_all[:, b, :], log_ratio[:, b : b + 1], q2_all[:, b, :], ALU.min, ALU.add
-            )
-            out_banks[b] = bank(f"d{b}", f"out_bank{b}")
-            for t in range(PACK):
-                nc.tensor.matmul(
-                    out_banks[b][:, t, :], mn[:, P * t : P * (t + 1)], ident[:],
-                    start=(t == 0), stop=False, is_transpose=True,
-                )
+                tanh_banks[b] = turn(sg[b], f"a{b}", f"tanh_bank{b}")
+            elif step[0] == "m":
+                minimum(b, gap[0][:, b, :])
+            else:
+                minimum(b, late.tile([P, N], F32, name=f"mn{b}", offset=(CHUNKS + b) * SLOT)[:])
 
         lg_all = late.tile([P, CHUNKS, N], F32, name="lg_all", offset=0)
         words = keep.tile([P, S], U32, name="words", align_bytes=64)
@@ -317,33 +340,28 @@ def tile_picked_gmm8_none_po_kernel(
         out_rows = out_0.rearrange("(p t) j -> p t j", t=PACK)
         out_words = out_1[0].rearrange("p n t -> p (n t)").bitcast(I32)
         for b in range(CHUNKS):
+            nc.scalar.activation(lg_all[:, b, :], flat(tanh_banks[b]), ACT.Ln, bias=1.0)
+        res, rounded = {}, {}
+        for step in OUT_ORDER.split():
+            b = int(step[1])
             cols = slice(CHUNK * b, CHUNK * (b + 1))
-            lg = lg_all[:, b, :]
-            nc.scalar.activation(lg, sg[b], ACT.Ln, scale=half_inv[:, b : b + 1], bias=half_inv[:, b : b + 1])
-            for t in range(PACK):
-                nc.tensor.matmul(
-                    out_banks[b][:, t, :], lg[:, P * t : P * (t + 1)], ident[:], start=False, stop=(t == PACK - 1), is_transpose=True
+            if step[0] == "r":
+                res[b] = slot(f"res{b}", f"res{b}")
+                nc.vector.scalar_tensor_tensor(flat(res[b]), flat(out_banks[b]), -1.0, lg_all[:, b, :], ALU.mult, ALU.subtract)
+                nc.sync.dma_start(out_rows[:, :, cols], res[b][:])
+            if step[0] == "b":
+                rounded[b] = work.tile([P, CHUNK, PACK], BF16, name=f"rounded{b}", align_bytes=64)
+                if ROUND_S[b]:
+                    nc.scalar.copy(rounded[b][:], res[b][:].rearrange("p t j -> p j t"))
+                else:
+                    nc.vector.tensor_copy(rounded[b][:], res[b][:].rearrange("p t j -> p j t"))
+            if step[0] == "q":
+                nc.vector.quantize_mx(
+                    out=words[:, cols].bitcast(FP8X4),
+                    scales=scales[:, cols],
+                    in_=rounded[b][:].rearrange("p j t -> p (j t)"),
                 )
-            res = slot(f"res{b}", f"res{b}")
-            if RES_S[b]:
-                nc.scalar.activation(flat(res), flat(out_banks[b]), ACT.Copy, scale=-1.0)
-            else:
-                nc.vector.tensor_scalar(flat(res), flat(out_banks[b]), -1.0, None, ALU.mult)
-            nc.sync.dma_start(out_rows[:, :, cols], res[:])
-            rounded = work.tile([P, CHUNK, PACK], BF16, name=f"rounded{b}", align_bytes=64)
-            if ROUND_S[b]:
-                nc.scalar.copy(rounded[:], res[:].rearrange("p t j -> p j t"))
-            else:
-                nc.vector.tensor_copy(rounded[:], res[:].rearrange("p t j -> p j t"))
-            nc.vector.quantize_mx(
-                out=words[:, cols].bitcast(FP8X4),
-                scales=scales[:, cols],
-                in_=rounded[:].rearrange("p j t -> p (j t)"),
-            )
-            if b == CHUNKS - 2:
-                nc.scalar.dma_start(out_words[:, 0 : CHUNK * (b + 1)], words[:, 0 : CHUNK * (b + 1)].bitcast(I32))
-            if b == CHUNKS - 1:
-                nc.sync.dma_start(out_words[:, cols], words[:, cols].bitcast(I32))
+        nc.sync.dma_start(out_words, words[:].bitcast(I32))
         for q in range(4):
             queue = nc.scalar if q % 2 == 0 else nc.sync
             queue.dma_start(

@@ -19,34 +19,13 @@ ALU = mybir.AluOpType
 
 P = 128
 PACK = 4
+QUADS = 4
 CHUNK = 128
 CHUNKS = S // CHUNK
+LAST = CHUNKS - 1
 LIST_COLS = CHUNK // 16
-HALF = N // 2
-SLOT = 4 * N
-CAST_S = (1, 1, 1, 0)
-CCOPY_S = (1, 1, 1, 1)
-ABS_S = (1, 1, 0, 0)
-ROUND_S = (1, 1, 0, 0)
-RES_S = (0, 0, 1, 1)
-QSPLIT = 2
-HOLD_WORDS = 2
-W1_HALVES = 0
-W2_HALVES = 1
-SPLIT_LAST = 0
-WIDE0 = 0
-ORDER = "c p o x s a b 1 k"
-V_ON_G = 0
-YBANKS = 4
-YEARLY = 4
-OUT_ORDER = "r0 r1 r2 r3 b0 b1 b2 b3 q0 q1 q2 q3"
-WARM = 1
-W1_SPLIT = 40
-CLOCKS = 0
-W1_SHARES = 1
-PLAN = "g020_s0 g021_x g220_s0 v0 g211_q00 v1 g311_q10 m0_00 v2 v3"
-GAP_ORDER = "a0 a1 m1 a2 a3 n2 n3"
-GS = (0, 1, 2, 0)
+W1_ON_SCALAR = 40
+SCALAR_CHUNKS = 2
 
 
 def tile_picked_gmm8_none_po_kernel(
@@ -54,18 +33,8 @@ def tile_picked_gmm8_none_po_kernel(
 ):
     nc = tc.nc
     with ExitStack() as ctx:
-        keep = ctx.enter_context(tc.tile_pool(name="keep", bufs=1))
-        reuse = ctx.enter_context(tc.tile_pool(name="reuse", bufs=1))
-        work = ctx.enter_context(tc.tile_pool(name="work", bufs=1))
-        held = ctx.enter_context(tc.tile_pool(name="held", bufs=1))
-        late = ctx.enter_context(tc.tile_pool(name="late", bufs=1))
+        sbuf = ctx.enter_context(tc.tile_pool(name="sbuf", bufs=1))
         psum = ctx.enter_context(tc.psum_pool(name="psum", bufs=1))
-
-        def slot(tag, name):
-            return work.tile([P, PACK, CHUNK], F32, name=name, tag=tag)
-
-        def placed(name, offset, width=CHUNK):
-            return held.tile([P, PACK, width], F32, name=name, offset=offset)
 
         def bank(tag, name):
             return psum.tile([P, PACK, CHUNK], F32, name=name, tag=tag)
@@ -73,297 +42,236 @@ def tile_picked_gmm8_none_po_kernel(
         def flat(tile):
             return tile[:].rearrange("p t j -> p (t j)")
 
-        pi_rows = keep.tile([P, P], F32, name="pi_rows")
+        pi_rows = sbuf.tile([P, P], F32, name="pi_rows")
         nc.gpsimd.memset(pi_rows[:], 0.0)
-        xs = keep.tile([P, T], U8, name="xs", align_bytes=64)
-        nc.vector.memset(xs[:].bitcast(I32), 0)
-        ident = keep.tile([P, P], F32, name="ident")
+        x_scales_sb = sbuf.tile([P, T], U8, name="x_scales_sb", align_bytes=64)
+        nc.vector.memset(x_scales_sb[:].bitcast(I32), 0)
+        ident = sbuf.tile([P, P], F32, name="ident")
         make_identity(nc, ident[:])
 
-        cen_sb = keep.tile([P, V // 16], U16, name="cen_sb")
-        offs_sb = keep.tile([P, S // 16], U16, name="offs_sb")
-        k_sb = [keep.tile([P, S // 16], U16, name=f"k{i + 1}_sb") for i in range(2)]
-        xw = keep.tile([P, T], I32, name="xw", align_bytes=64)
-        if W2_HALVES:
-            w2_raw = [keep.tile([P, PACK, HALF], F32, name=f"w2_raw{h}") for h in range(2)]
-        else:
-            w2_whole = keep.tile([P, PACK, N], F32, name="w2_whole")
-            w2_raw = [w2_whole[:, :, HALF * h : HALF * (h + 1)] for h in range(2)]
-        if W1_HALVES:
-            w1_raw = [keep.tile([P, PACK, HALF], F32, name=f"w1_raw{h}") for h in range(2)]
-        else:
-            w1_whole = keep.tile([P, PACK, N], F32, name="w1_whole")
-            w1_raw = [w1_whole[:, :, HALF * h : HALF * (h + 1)] for h in range(2)]
+        cen_sb = sbuf.tile([P, V // 16], U16, name="cen_sb")
+        nc.sync.dma_start(cen_sb[:], cen)
+        for i, pi in enumerate((pi1, pi2)):
+            nc.scalar.dma_start(
+                pi_rows[CHUNKS * i : CHUNKS * (i + 1), :], pi[0:1, :].rearrange("o (b j) -> (o b) j", b=CHUNKS)
+            )
+        offs_sb = sbuf.tile([P, S // 16], U16, name="offs_sb")
+        nc.sync.dma_start(offs_sb[:], offs)
+        x_words_sb = sbuf.tile([P, T], I32, name="x_words_sb", align_bytes=64)
+        nc.sync.dma_start(x_words_sb[:], x_words[0].rearrange("p n r -> p (n r)").bitcast(I32))
+        for q in range(QUADS):
+            nc.sync.dma_start(
+                x_scales_sb[32 * q : 32 * q + 4, :].bitcast(I32), x_scales[0, 4 * q : 4 * q + 4, :].bitcast(I32)
+            )
+        w2_raw = []
+        for h in range(2):
+            raw = sbuf.tile([P, PACK, N // 2], F32, name=f"w2_raw{h}")
+            nc.sync.dma_start(raw[:], w2.rearrange("(p r) m -> p r m", r=PACK)[:, :, N // 2 * h : N // 2 * (h + 1)])
+            w2_raw.append(raw)
+        w1_raw = sbuf.tile([P, PACK, N], F32, name="w1_raw")
+        nc.sync.dma_start(w1_raw[:], w1.rearrange("(p r) m -> p r m", r=PACK))
+        k_sb = []
+        for i, lists in enumerate((k1, k2)):
+            lists_sb = sbuf.tile([P, S // 16], U16, name=f"k{i + 1}_sb")
+            nc.sync.dma_start(lists_sb[:], lists)
+            k_sb.append(lists_sb)
 
-        def half(w, h):
-            return w.rearrange("(p j) m -> p j m", j=PACK)[:, :, HALF * h : HALF * (h + 1)]
-
-        for what in ORDER.split():
-            if what == "c":
-                nc.sync.dma_start(cen_sb[:], cen)
-            if what == "o":
-                nc.sync.dma_start(offs_sb[:], offs)
-            if what == "k":
-                nc.sync.dma_start(k_sb[0][:], k1)
-                nc.sync.dma_start(k_sb[1][:], k2)
-            if what == "p":
-                for i, pi in enumerate((pi1, pi2)):
-                    nc.scalar.dma_start(
-                        pi_rows[CHUNKS * i : CHUNKS * (i + 1), :], pi[0:1, :].rearrange("o (b q) -> (o b) q", b=CHUNKS)
-                    )
-            if what == "x":
-                nc.sync.dma_start(xw[:], x_words[0].rearrange("p n t -> p (n t)").bitcast(I32))
-            if what == "s":
-                for q in range(4):
-                    nc.sync.dma_start(
-                        xs[32 * q : 32 * q + 4, :].bitcast(I32), x_scales[0, 4 * q : 4 * q + 4, :].bitcast(I32)
-                    )
-            if what == "a" and not W2_HALVES:
-                nc.sync.dma_start(w2_whole[:], w2.rearrange("(p j) m -> p j m", j=PACK))
-            if what == "a" and W2_HALVES:
-                nc.sync.dma_start(w2_raw[0][:], half(w2, 0))
-            if what == "b" and W2_HALVES:
-                nc.sync.dma_start(w2_raw[1][:], half(w2, 1))
-            if what == "1":
-                if W1_HALVES:
-                    for h in range(2):
-                        nc.sync.dma_start(w1_raw[h][:], half(w1, h))
-                else:
-                    nc.sync.dma_start(w1_whole[:], w1.rearrange("(p j) m -> p j m", j=PACK))
-
-        pi_bank = bank("d0", "pi_bank")
+        pi_bank = bank("b0", "pi_bank")
         nc.tensor.transpose(pi_bank[:, 0, :], pi_rows[:], ident[:])
-        log_pi = keep.tile([P, 2 * CHUNKS], F32, name="log_pi")
+        log_pi = sbuf.tile([P, 2 * CHUNKS], F32, name="log_pi")
         nc.scalar.activation(log_pi[:], pi_bank[:, 0, 0 : 2 * CHUNKS], ACT.Ln, scale=2.0)
-        limit = keep.tile([P, CHUNKS], F32, name="limit")
-        nc.scalar.activation(limit[:], log_pi[:, CHUNKS : 2 * CHUNKS], ACT.Copy, scale=-1.0)
-        tanh_bias = late.tile([P, CHUNKS], F32, name="tanh_bias", offset=0)
-        nc.scalar.activation(tanh_bias[:], log_pi[:, CHUNKS : 2 * CHUNKS], ACT.Copy, scale=0.5)
-        if WARM:
-            warm = reuse.tile([P, 1], F32, name="warm", align_bytes=64, offset=0)
-            nc.scalar.activation(warm[:], log_pi[:, 0:1], ACT.Tanh)
+        neg_l2 = sbuf.tile([P, CHUNKS], F32, name="neg_l2")
+        nc.scalar.activation(neg_l2[:], log_pi[:, CHUNKS : 2 * CHUNKS], ACT.Copy, scale=-1.0)
+        half_l2 = sbuf.tile([P, CHUNKS], F32, name="half_l2", tag="half_l2")
+        nc.scalar.activation(half_l2[:], log_pi[:, CHUNKS : 2 * CHUNKS], ACT.Copy, scale=0.5)
+        warm_up = sbuf.tile([P, 1], F32, name="warm_up", tag="rounded_w", align_bytes=64)
+        nc.scalar.activation(warm_up[:], log_pi[:, 0:1], ACT.Tanh)
 
-        def gather_columns(lst, words, scales):
-            nc.vector.tensor_copy(words[:], xw[:].bitcast(U32).indirect(lst[:]))
-            nc.vector.tensor_copy(scales[:], xs[:].indirect(lst[:]))
+        def gather_words(name, lst):
+            picked = sbuf.tile([P, S], U32, name=name, tag=name, align_bytes=64)
+            nc.vector.tensor_copy(picked[:], x_words_sb[:].bitcast(U32).indirect(lst[:]))
+            return picked
 
-        def round_half(raw, grouped, h, on_scalar):
-            dst = grouped[:, :, 64 * h : 64 * (h + 1), :].rearrange("p t m j -> p m t j")
-            src = raw[:].rearrange("p j (m t) -> p m t j", t=PACK)
-            if on_scalar:
-                nc.scalar.copy(dst, src)
-            else:
-                nc.vector.tensor_copy(dst, src)
+        def gather_scales(name, lst):
+            picked = sbuf.tile([P, S], U8, name=name, align_bytes=64)
+            nc.vector.tensor_copy(picked[:], x_scales_sb[:].indirect(lst[:]))
+            return picked
 
-        def round_part(lo, hi, grouped, on_scalar):
-            dst = grouped[:, :, lo:hi, :].rearrange("p t m j -> p m t j")
-            src = w1_whole[:, :, PACK * lo : PACK * hi].rearrange("p j (m t) -> p m t j", t=PACK)
-            if on_scalar:
-                nc.scalar.copy(dst, src)
-            else:
-                nc.vector.tensor_copy(dst, src)
+        def round_weight(copy, rounded, lo, hi, raw):
+            copy(rounded[:, :, lo:hi, :].rearrange("p t m r -> p m t r"), raw.rearrange("p r (m t) -> p m t r", t=PACK))
 
-        def quantise_weight(grouped, name):
-            codes = keep.tile([P, PACK, P], U32, name=f"{name}_codes", align_bytes=64)
-            scales = keep.tile([P, PACK, P], U8, name=f"{name}_scales", align_bytes=64)
-            step = PACK // QSPLIT
-            for t in range(0, PACK, step):
+        def quantise_weight(name, rounded):
+            codes = sbuf.tile([P, PACK, P], U32, name=f"{name}_codes", align_bytes=64)
+            scales = sbuf.tile([P, PACK, P], U8, name=f"{name}_scales", align_bytes=64)
+            for t in range(0, PACK, 2):
                 nc.vector.quantize_mx(
-                    out=codes[:, t : t + step, :].rearrange("p t m -> p (t m)").bitcast(FP8X4),
-                    scales=scales[:, t : t + step, :].rearrange("p t m -> p (t m)"),
-                    in_=grouped[:, t : t + step, :, :].rearrange("p t m j -> p (t m j)"),
+                    out=codes[:, t : t + 2, :].rearrange("p t m -> p (t m)").bitcast(FP8X4),
+                    scales=scales[:, t : t + 2, :].rearrange("p t m -> p (t m)"),
+                    in_=rounded[:, t : t + 2, :, :].rearrange("p t m r -> p (t m r)"),
                 )
             return codes, scales
 
-        xc_words = keep.tile([P, V], U32, name="xc_words", align_bytes=64)
-        xc_scales = keep.tile([P, V], U8, name="xc_scales", align_bytes=64)
-        gather_columns(cen_sb, xc_words, xc_scales)
-        w2_grouped = reuse.tile([P, PACK, P, PACK], BF16, name="w2_grouped", align_bytes=64, offset=0)
-        round_half(w2_raw[0], w2_grouped, 0, CAST_S[0])
-        round_half(w2_raw[1], w2_grouped, 1, CAST_S[1])
-        if CLOCKS:
-            clock = keep.tile([P, 2], F32, name="clock")
-            nc.gpsimd.tensor_copy(clock[:, 1:2], w2_grouped[:, 3, 127, 0:1])
-        w2_codes, w2_scales = quantise_weight(w2_grouped, "w2")
-        w1_grouped = reuse.tile([P, PACK, P, PACK], BF16, name="w1_grouped", align_bytes=64, offset=0 if W1_SHARES else 16 * S)
-        if CAST_S[2]:
-            round_part(0, W1_SPLIT, w1_grouped, True)
-        if CAST_S[3] == 1:
-            round_half(w1_raw[1], w1_grouped, 1, True)
-        neg_c = []
-        for t in range(PACK):
-            c_bank = bank(f"a{t}", f"c_bank{t}")
+        def product(out, w_codes, w_scales, t, words, scales):
             nc.tensor.matmul_mx(
-                out=flat(c_bank),
-                lhsT=w2_codes[:, t, :].bitcast(FP8X4),
-                lhsT_scale=w2_scales[:, t, :],
-                rhs=xc_words[:].bitcast(FP8X4),
-                rhs_scale=xc_scales[:],
+                out=out,
+                lhsT=w_codes[:, t, :].bitcast(FP8X4),
+                lhsT_scale=w_scales[:, t, :],
+                rhs=words.bitcast(FP8X4),
+                rhs_scale=scales,
                 start=True,
                 stop=True,
             )
-            window = keep.tile([P, V], F32, name=f"neg_c{t}")
-            if CCOPY_S[t]:
-                nc.scalar.activation(window[:], flat(c_bank), ACT.Copy, scale=-1.0)
-            else:
-                nc.vector.tensor_scalar(window[:], flat(c_bank), -1.0, None, ALU.mult)
+
+        cen_words = gather_words("cen_words", cen_sb)
+        offs_words = gather_words("offs_words", offs_sb)
+        cen_scales = gather_scales("cen_scales", cen_sb)
+        w2_rounded = sbuf.tile([P, PACK, P, PACK], BF16, name="w2_rounded", tag="rounded_w", align_bytes=64)
+        for h in range(2):
+            round_weight(nc.scalar.copy, w2_rounded, P // 2 * h, P // 2 * (h + 1), w2_raw[h][:])
+        w2_codes, w2_scales = quantise_weight("w2", w2_rounded)
+        w1_rounded = sbuf.tile([P, PACK, P, PACK], BF16, name="w1_rounded", tag="rounded_w", align_bytes=64)
+        round_weight(nc.scalar.copy, w1_rounded, 0, W1_ON_SCALAR, w1_raw[:, :, 0 : PACK * W1_ON_SCALAR])
+        neg_c = []
+        for t in range(PACK):
+            c_bank = bank(f"a{t}", f"c_bank{t}")
+            product(flat(c_bank), w2_codes, w2_scales, t, cen_words[:], cen_scales[:])
+            window = sbuf.tile([P, V], F32, name=f"neg_c{t}")
+            nc.scalar.activation(window[:], flat(c_bank), ACT.Copy, scale=-1.0)
             neg_c.append(window)
 
-        xo_words = reuse.tile([P, S], U32, name="xo_words", align_bytes=64, offset=0 if HOLD_WORDS == 1 else 8 * S)
-        xo_scales = reuse.tile([P, S], U8, name="xo_scales", align_bytes=64, offset=12 * S)
-        gather_columns(offs_sb, xo_words, xo_scales)
-        if not CAST_S[2]:
-            round_half(w1_raw[0], w1_grouped, 0, False)
-        if CAST_S[3] != 1:
-            round_part(W1_SPLIT, P, w1_grouped, False)
-        w1_codes, w1_scales = quantise_weight(w1_grouped, "w1")
+        offs_scales = gather_scales("offs_scales", offs_sb)
+        round_weight(nc.vector.tensor_copy, w1_rounded, W1_ON_SCALAR, P, w1_raw[:, :, PACK * W1_ON_SCALAR : N])
+        w1_codes, w1_scales = quantise_weight("w1", w1_rounded)
         y_banks = []
-
-        def project(b):
-            y_bank = bank(f"d{b % YBANKS}", f"y_bank{b}")
+        for b in range(CHUNKS):
+            y_bank = bank(f"b{b}", f"y_bank{b}")
             cols = slice(CHUNK * b, CHUNK * (b + 1))
             for t in range(PACK):
-                nc.tensor.matmul_mx(
-                    out=y_bank[:, t, :],
-                    lhsT=w1_codes[:, t, :].bitcast(FP8X4),
-                    lhsT_scale=w1_scales[:, t, :],
-                    rhs=xo_words[:, cols].bitcast(FP8X4),
-                    rhs_scale=xo_scales[:, cols],
-                    start=True,
-                    stop=True,
-                )
+                product(y_bank[:, t, :], w1_codes, w1_scales, t, offs_words[:, cols], offs_scales[:, cols])
             y_banks.append(y_bank)
+        y = []
+        for b in range(CHUNKS):
+            y_chunk = sbuf.tile([P, PACK, CHUNK], F32, name=f"y{b}")
+            nc.scalar.copy(flat(y_chunk), flat(y_banks[b]))
+            y.append(y_chunk)
 
-        for b in range(YEARLY):
-            project(b)
-        q2_all = keep.tile([P, CHUNKS, N], F32, name="q2_all")
-        v_all = keep.tile([P, CHUNKS, N], F32, name="v_all")
-        th_all = late.tile([P, CHUNKS, N], F32, name="th_all", offset=CHUNKS * SLOT)
-        q1, sg, gap, out_banks, tanh_banks = {}, {}, [], {}, {}
+        q1 = {}
+        q2 = sbuf.tile([P, CHUNKS, N], F32, name="q2")
+        diff = sbuf.tile([P, CHUNKS, N], F32, name="diff")
+        tanh = sbuf.tile([P, CHUNKS, N], F32, name="tanh", tag="tanh")
+        abs_tanh = {}
 
-        ys = {}
-        y_pairs = [keep.tile([P, PACK, 2 * CHUNK], F32, name=f"y{h}") for h in range(2)]
-
-        def y_copy(b):
-            ys[b] = y_pairs[b // 2][:, :, CHUNK * (b % 2) : CHUNK * (b % 2 + 1)]
-            nc.scalar.copy(ys[b], y_banks[b][:])
-
-        def distances(b0, n, i, hold, fused):
-            name = f"g{i}_{b0}"
-            if hold == "x":
-                g = reuse.tile([P, PACK, n * CHUNK], F32, name=name, align_bytes=64, offset=8 * S)
-            elif hold[0] == "s":
-                g = work.tile([P, PACK, n * CHUNK], F32, name=name, tag=hold)
-            else:
-                g = placed(name, 2 * SLOT * int(hold[1]) + SLOT * int(hold[2]), n * CHUNK)
+        def squared_distances(i, first, count, tag, parts):
+            looked_up = sbuf.tile([P, PACK, count * CHUNK], F32, name=f"c{i + 1}_{first}", tag=tag, align_bytes=64)
+            entries = k_sb[i][:, LIST_COLS * first : LIST_COLS * (first + count)]
             d_banks = []
-            for b in range(b0, b0 + n):
-                if b not in ys:
-                    y_copy(b)
-                d_bank = bank(f"a{count[0] % 4}", f"d_bank{i}_{b}")
-                count.insert(0, count[0] + 1)
-                for t in range(0 if fused else PACK):
-                    nc.tensor.matmul(d_bank[:, t, :], ys[b][:, t, :], ident[:], start=(t == 0), stop=False, is_transpose=True)
+            for bank_tag, b, tiles, dst in parts:
+                d_bank = bank(bank_tag, f"d_bank_{bank_tag}")
+                for t in tiles:
+                    nc.tensor.matmul(
+                        d_bank[:, t, :], y[b][:, t, :], ident[:], start=(t == tiles[0]), stop=False, is_transpose=True
+                    )
                 d_banks.append(d_bank)
             for t in range(PACK):
-                looked_up = neg_c[t][:].indirect(k_sb[i][:, LIST_COLS * b0 : LIST_COLS * (b0 + n)])
-                if fused:
-                    first = CHUNK * (b0 % 2)
-                    nc.vector.tensor_tensor(g[:, t, :], looked_up, y_pairs[b0 // 2][:, t, first : first + n * CHUNK], ALU.add)
-                else:
-                    nc.vector.tensor_copy(g[:, t, :], looked_up)
-                for u in range(n):
-                    nc.tensor.matmul(
-                        d_banks[u][:, t, :], g[:, t, CHUNK * u : CHUNK * (u + 1)], ident[:],
-                        start=(fused and t == 0), stop=(t == PACK - 1), is_transpose=True,
-                    )
-            for u in range(n):
-                b = b0 + u
-                if i == 0:
-                    q1[b] = placed(f"q1_{b}", 2 * SLOT * b + SLOT // 2)
-                    dst = flat(q1[b])
-                else:
-                    dst = q2_all[:, b, :]
-                nc.scalar.activation(dst, flat(d_banks[u]), ACT.Square, scale=math.sqrt(0.125))
+                nc.vector.tensor_copy(looked_up[:, t, :], neg_c[t][:].indirect(entries))
+                for d_bank, (bank_tag, b, tiles, dst) in zip(d_banks, parts):
+                    if t in tiles:
+                        block = looked_up[:, t, CHUNK * (b - first) : CHUNK * (b - first + 1)]
+                        nc.tensor.matmul(
+                            d_bank[:, t, :], block, ident[:], start=False, stop=(t == tiles[-1]), is_transpose=True
+                        )
+            for d_bank, (bank_tag, b, tiles, dst) in zip(d_banks, parts):
+                cols = slice(P * tiles[0], P * (tiles[-1] + 1))
+                nc.scalar.activation(dst[:, cols], flat(d_bank)[:, cols], ACT.Square, scale=math.sqrt(0.125))
 
-        count = [0]
+        def first_component(first, count, tag):
+            for b in range(first, first + count):
+                q1[b] = sbuf.tile([P, N], F32, name=f"q1_{b}", tag=f"q1_{b}", align_bytes=64)
+            parts = [(f"a{b % 2}", b, range(PACK), q1[b][:]) for b in range(first, first + count)]
+            squared_distances(0, first, count, tag, parts)
 
-        def exponentials(b):
+        def second_component(first, count, tag):
+            parts = [(f"a{2 + b % 2}", b, range(PACK), q2[:, b, :]) for b in range(first, first + count)]
+            squared_distances(1, first, count, tag, parts)
+
+        def difference_and_tanh(b, cols):
             nc.vector.scalar_tensor_tensor(
-                v_all[:, b, :], flat(q1[b]), log_pi[:, b : b + 1], q2_all[:, b, :], ALU.subtract, ALU.subtract
+                diff[:, b, cols], q1[b][:, cols], log_pi[:, b : b + 1], q2[:, b, cols], ALU.subtract, ALU.subtract
             )
-            nc.scalar.activation(th_all[:, b, :], v_all[:, b, :], ACT.Tanh, scale=0.5, bias=tanh_bias[:, b : b + 1])
-            if ABS_S[b]:
-                magnitude(b)
+            nc.scalar.activation(tanh[:, b, cols], diff[:, b, cols], ACT.Tanh, scale=0.5, bias=half_l2[:, b : b + 1])
 
-        def magnitude(b):
-            if ABS_S[b]:
-                sg[b] = flat(slot(f"sg{b}", f"sg{b}"))
-                nc.scalar.activation(sg[b], th_all[:, b, :], ACT.Abs)
-            else:
-                sg[b] = gap[0][:, CHUNKS + b, :]
-                nc.vector.scalar_tensor_tensor(sg[b], th_all[:, b, :], -1.0, th_all[:, b, :], ALU.mult, ALU.max)
+        def early_chunk_tanh(b):
+            difference_and_tanh(b, slice(0, N))
+            abs_tanh[b] = sbuf.tile([P, N], F32, name=f"abs_tanh{b}")[:]
+            nc.scalar.activation(abs_tanh[b], tanh[:, b, :], ACT.Abs)
 
-        def turn(src, tag, name):
+        def turn_back(src, tag, name):
             dst = bank(tag, name)
             for t in range(PACK):
                 nc.tensor.transpose(dst[:, t, :], src[:, P * t : P * (t + 1)], ident[:])
             return dst
 
-        def minimum(b, mn):
-            nc.vector.scalar_tensor_tensor(mn, v_all[:, b, :], limit[:, b : b + 1], q2_all[:, b, :], ALU.min, ALU.add)
-            out_banks[b] = turn(mn, f"d{b}", f"min_bank{b}")
+        min_banks = {}
 
-        for step in PLAN.split():
-            if step[0] == "v":
-                exponentials(int(step[1]))
-            elif step[0] == "m":
-                minimum(int(step[1]), flat(placed(step, 2 * SLOT * int(step[3]) + SLOT * int(step[4]))))
-            else:
-                distances(int(step[1]), int(step[2]), int(step[3]), step[5:], step[0] == "f")
+        def minimum(b, dst):
+            nc.vector.scalar_tensor_tensor(dst, diff[:, b, :], neg_l2[:, b : b + 1], q2[:, b, :], ALU.min, ALU.add)
+            min_banks[b] = turn_back(dst, f"b{b}", f"min_bank{b}")
 
-        gap.append(held.tile([P, 2 * CHUNKS, N], F32, name="gap", offset=2 * SLOT * (CHUNKS - 1) + SLOT // 2))
-        for step in GAP_ORDER.split():
-            b = int(step[1])
-            if step[0] == "a":
-                if not ABS_S[b]:
-                    magnitude(b)
-                tanh_banks[b] = turn(sg[b], f"a{b}", f"tanh_bank{b}")
-            elif step[0] == "m":
-                minimum(b, gap[0][:, b, :])
-            else:
-                minimum(b, late.tile([P, N], F32, name=f"mn{b}", offset=(CHUNKS + b) * SLOT)[:])
+        first_component(0, 2, "pair")
+        second_component(0, 2, "offs_words")
+        early_chunk_tanh(0)
+        first_component(2, 2, "pair")
+        early_chunk_tanh(1)
+        second_component(2, 1, "q1_0")
+        halves = [("a3", LAST, range(0, 2), q2[:, LAST, :]), ("a0", LAST, range(2, 4), q2[:, LAST, :])]
+        squared_distances(1, LAST, 1, "q1_1", halves)
+        minimum(0, sbuf.tile([P, N], F32, name="min0", tag="q1_0", align_bytes=64)[:])
+        difference_and_tanh(2, slice(0, N))
+        for h in range(2):
+            difference_and_tanh(LAST, slice(N // 2 * h, N // 2 * (h + 1)))
 
-        lg_all = late.tile([P, CHUNKS, N], F32, name="lg_all", offset=0)
-        words = keep.tile([P, S], U32, name="words", align_bytes=64)
-        scales = keep.tile([P, S], U8, name="scales", align_bytes=64)
-        out_rows = out_0.rearrange("(p t) j -> p t j", t=PACK)
-        out_words = out_1[0].rearrange("p n t -> p (n t)").bitcast(I32)
+        after_last = sbuf.tile([P, 3, N], F32, name="after_last", tag=f"q1_{LAST}", align_bytes=64)
+        tanh_banks = [turn_back(abs_tanh[b], f"a{b}", f"tanh_bank{b}") for b in range(SCALAR_CHUNKS)]
+        minimum(1, after_last[:, 0, :])
+        for b in range(SCALAR_CHUNKS, CHUNKS):
+            magnitude = after_last[:, b - 1, :]
+            nc.vector.scalar_tensor_tensor(magnitude, tanh[:, b, :], -1.0, tanh[:, b, :], ALU.mult, ALU.max)
+            tanh_banks.append(turn_back(magnitude, f"a{b}", f"tanh_bank{b}"))
+        last_mins = sbuf.tile([P, 2, N], F32, name="last_mins", tag="tanh")
+        for b in range(2, CHUNKS):
+            minimum(b, last_mins[:, b - 2, :])
+
+        logs = sbuf.tile([P, CHUNKS, N], F32, name="logs", tag="half_l2")
         for b in range(CHUNKS):
-            nc.scalar.activation(lg_all[:, b, :], flat(tanh_banks[b]), ACT.Ln, bias=1.0)
-        res, rounded = {}, {}
-        for step in OUT_ORDER.split():
-            b = int(step[1])
-            cols = slice(CHUNK * b, CHUNK * (b + 1))
-            if step[0] == "r":
-                res[b] = slot(f"res{b}", f"res{b}")
-                nc.vector.scalar_tensor_tensor(flat(res[b]), flat(out_banks[b]), -1.0, lg_all[:, b, :], ALU.mult, ALU.subtract)
-                nc.sync.dma_start(out_rows[:, :, cols], res[b][:])
-            if step[0] == "b":
-                rounded[b] = work.tile([P, CHUNK, PACK], BF16, name=f"rounded{b}", align_bytes=64)
-                if ROUND_S[b]:
-                    nc.scalar.copy(rounded[b][:], res[b][:].rearrange("p t j -> p j t"))
-                else:
-                    nc.vector.tensor_copy(rounded[b][:], res[b][:].rearrange("p t j -> p j t"))
-            if step[0] == "q":
+            nc.scalar.activation(logs[:, b, :], flat(tanh_banks[b]), ACT.Ln, bias=1.0)
+        out_rows = out_0.rearrange("(p t) j -> p t j", t=PACK)
+        results = []
+        for b in range(CHUNKS):
+            result = sbuf.tile([P, PACK, CHUNK], F32, name=f"result{b}")
+            nc.vector.scalar_tensor_tensor(flat(result), flat(min_banks[b]), -1.0, logs[:, b, :], ALU.mult, ALU.subtract)
+            nc.sync.dma_start(out_rows[:, :, CHUNK * b : CHUNK * (b + 1)], result[:])
+            results.append(result)
+        rounded_out = []
+        for b in range(CHUNKS):
+            rounded = sbuf.tile([P, CHUNK, PACK], BF16, name=f"rounded_out{b}", align_bytes=64)
+            copy = nc.scalar.copy if b < SCALAR_CHUNKS else nc.vector.tensor_copy
+            copy(rounded[:], results[b][:].rearrange("p t j -> p j t"))
+            rounded_out.append(rounded)
+        out_codes = sbuf.tile([P, S], U32, name="out_codes", align_bytes=64)
+        out_scales = sbuf.tile([P, S], U8, name="out_scales", align_bytes=64)
+        out_words = out_1[0].rearrange("p n r -> p (n r)").bitcast(I32)
+        for half in range(2):
+            for b in (2 * half, 2 * half + 1):
+                cols = slice(CHUNK * b, CHUNK * (b + 1))
                 nc.vector.quantize_mx(
-                    out=words[:, cols].bitcast(FP8X4),
-                    scales=scales[:, cols],
-                    in_=rounded[b][:].rearrange("p j t -> p (j t)"),
+                    out=out_codes[:, cols].bitcast(FP8X4),
+                    scales=out_scales[:, cols],
+                    in_=rounded_out[b][:].rearrange("p j t -> p (j t)"),
                 )
-        nc.sync.dma_start(out_words, words[:].bitcast(I32))
-        for q in range(4):
+            cols = slice(S // 2 * half, S // 2 * (half + 1))
+            nc.sync.dma_start(out_words[:, cols], out_codes[:, cols].bitcast(I32))
+        for q in range(QUADS):
             queue = nc.scalar if q % 2 == 0 else nc.sync
             queue.dma_start(
-                out_2[0, 4 * q : 4 * q + 4, :].bitcast(I32), scales[32 * q : 32 * q + 4, :].bitcast(I32)
+                out_2[0, 4 * q : 4 * q + 4, :].bitcast(I32), out_scales[32 * q : 32 * q + 4, :].bitcast(I32)
             )

import math
from contextlib import ExitStack

import concourse.mybir as mybir
from concourse.masks import make_identity

K, T, S, V, N = 512, 2048, 512, 512, 512
FLOPS = 2 * K * N * (S + V)

F32 = mybir.dt.float32
BF16 = mybir.dt.bfloat16
I32 = mybir.dt.int32
U32 = mybir.dt.uint32
U16 = mybir.dt.uint16
U8 = mybir.dt.uint8
FP8X4 = mybir.dt.float8_e4m3fn_x4
ACT = mybir.ActivationFunctionType
ALU = mybir.AluOpType

P = 128
PACK = 4
QUADS = 4
CHUNK = 128
CHUNKS = S // CHUNK
LAST = CHUNKS - 1
LIST_COLS = CHUNK // 16
W1_ON_SCALAR = 40
SCALAR_CHUNKS = 2


def tile_picked_gmm8_none_po_kernel(
    tc, x_words, x_scales, w1, w2, pi1, pi2, offs, cen, k1, k2, out_0, out_1, out_2
):
    nc = tc.nc
    with ExitStack() as ctx:
        sbuf = ctx.enter_context(tc.tile_pool(name="sbuf", bufs=1))
        psum = ctx.enter_context(tc.psum_pool(name="psum", bufs=1))

        def bank(tag, name):
            return psum.tile([P, PACK, CHUNK], F32, name=name, tag=tag)

        def flat(tile):
            return tile[:].rearrange("p t j -> p (t j)")

        pi_rows = sbuf.tile([P, P], F32, name="pi_rows")
        nc.gpsimd.memset(pi_rows[:], 0.0)
        x_scales_sb = sbuf.tile([P, T], U8, name="x_scales_sb", align_bytes=64)
        nc.vector.memset(x_scales_sb[:].bitcast(I32), 0)
        ident = sbuf.tile([P, P], F32, name="ident")
        make_identity(nc, ident[:])

        cen_sb = sbuf.tile([P, V // 16], U16, name="cen_sb")
        nc.sync.dma_start(cen_sb[:], cen)
        for i, pi in enumerate((pi1, pi2)):
            nc.scalar.dma_start(
                pi_rows[CHUNKS * i : CHUNKS * (i + 1), :], pi[0:1, :].rearrange("o (b j) -> (o b) j", b=CHUNKS)
            )
        offs_sb = sbuf.tile([P, S // 16], U16, name="offs_sb")
        nc.sync.dma_start(offs_sb[:], offs)
        x_words_sb = sbuf.tile([P, T], I32, name="x_words_sb", align_bytes=64)
        nc.sync.dma_start(x_words_sb[:], x_words[0].rearrange("p n r -> p (n r)").bitcast(I32))
        for q in range(QUADS):
            nc.sync.dma_start(
                x_scales_sb[32 * q : 32 * q + 4, :].bitcast(I32), x_scales[0, 4 * q : 4 * q + 4, :].bitcast(I32)
            )
        w2_raw = []
        for h in range(2):
            raw = sbuf.tile([P, PACK, N // 2], F32, name=f"w2_raw{h}")
            nc.sync.dma_start(raw[:], w2.rearrange("(p r) m -> p r m", r=PACK)[:, :, N // 2 * h : N // 2 * (h + 1)])
            w2_raw.append(raw)
        w1_raw = sbuf.tile([P, PACK, N], F32, name="w1_raw")
        nc.sync.dma_start(w1_raw[:], w1.rearrange("(p r) m -> p r m", r=PACK))
        k_sb = []
        for i, lists in enumerate((k1, k2)):
            lists_sb = sbuf.tile([P, S // 16], U16, name=f"k{i + 1}_sb")
            nc.sync.dma_start(lists_sb[:], lists)
            k_sb.append(lists_sb)

        pi_bank = bank("b0", "pi_bank")
        nc.tensor.transpose(pi_bank[:, 0, :], pi_rows[:], ident[:])
        log_pi = sbuf.tile([P, 2 * CHUNKS], F32, name="log_pi")
        nc.scalar.activation(log_pi[:], pi_bank[:, 0, 0 : 2 * CHUNKS], ACT.Ln, scale=2.0)
        neg_l2 = sbuf.tile([P, CHUNKS], F32, name="neg_l2")
        nc.scalar.activation(neg_l2[:], log_pi[:, CHUNKS : 2 * CHUNKS], ACT.Copy, scale=-1.0)
        half_l2 = sbuf.tile([P, CHUNKS], F32, name="half_l2", tag="half_l2")
        nc.scalar.activation(half_l2[:], log_pi[:, CHUNKS : 2 * CHUNKS], ACT.Copy, scale=0.5)
        warm_up = sbuf.tile([P, 1], F32, name="warm_up", tag="rounded_w", align_bytes=64)
        nc.scalar.activation(warm_up[:], log_pi[:, 0:1], ACT.Tanh)

        def gather_words(name, lst):
            picked = sbuf.tile([P, S], U32, name=name, tag=name, align_bytes=64)
            nc.vector.tensor_copy(picked[:], x_words_sb[:].bitcast(U32).indirect(lst[:]))
            return picked

        def gather_scales(name, lst):
            picked = sbuf.tile([P, S], U8, name=name, align_bytes=64)
            nc.vector.tensor_copy(picked[:], x_scales_sb[:].indirect(lst[:]))
            return picked

        def round_weight(copy, rounded, lo, hi, raw):
            copy(rounded[:, :, lo:hi, :].rearrange("p t m r -> p m t r"), raw.rearrange("p r (m t) -> p m t r", t=PACK))

        def quantise_weight(name, rounded):
            codes = sbuf.tile([P, PACK, P], U32, name=f"{name}_codes", align_bytes=64)
            scales = sbuf.tile([P, PACK, P], U8, name=f"{name}_scales", align_bytes=64)
            for t in range(0, PACK, 2):
                nc.vector.quantize_mx(
                    out=codes[:, t : t + 2, :].rearrange("p t m -> p (t m)").bitcast(FP8X4),
                    scales=scales[:, t : t + 2, :].rearrange("p t m -> p (t m)"),
                    in_=rounded[:, t : t + 2, :, :].rearrange("p t m r -> p (t m r)"),
                )
            return codes, scales

        def product(out, w_codes, w_scales, t, words, scales):
            nc.tensor.matmul_mx(
                out=out,
                lhsT=w_codes[:, t, :].bitcast(FP8X4),
                lhsT_scale=w_scales[:, t, :],
                rhs=words.bitcast(FP8X4),
                rhs_scale=scales,
                start=True,
                stop=True,
            )

        cen_words = gather_words("cen_words", cen_sb)
        offs_words = gather_words("offs_words", offs_sb)
        cen_scales = gather_scales("cen_scales", cen_sb)
        w2_rounded = sbuf.tile([P, PACK, P, PACK], BF16, name="w2_rounded", tag="rounded_w", align_bytes=64)
        for h in range(2):
            round_weight(nc.scalar.copy, w2_rounded, P // 2 * h, P // 2 * (h + 1), w2_raw[h][:])
        w2_codes, w2_scales = quantise_weight("w2", w2_rounded)
        w1_rounded = sbuf.tile([P, PACK, P, PACK], BF16, name="w1_rounded", tag="rounded_w", align_bytes=64)
        round_weight(nc.scalar.copy, w1_rounded, 0, W1_ON_SCALAR, w1_raw[:, :, 0 : PACK * W1_ON_SCALAR])
        neg_c = []
        for t in range(PACK):
            c_bank = bank(f"a{t}", f"c_bank{t}")
            product(flat(c_bank), w2_codes, w2_scales, t, cen_words[:], cen_scales[:])
            window = sbuf.tile([P, V], F32, name=f"neg_c{t}")
            nc.scalar.activation(window[:], flat(c_bank), ACT.Copy, scale=-1.0)
            neg_c.append(window)

        offs_scales = gather_scales("offs_scales", offs_sb)
        round_weight(nc.vector.tensor_copy, w1_rounded, W1_ON_SCALAR, P, w1_raw[:, :, PACK * W1_ON_SCALAR : N])
        w1_codes, w1_scales = quantise_weight("w1", w1_rounded)
        y_banks = []
        for b in range(CHUNKS):
            y_bank = bank(f"b{b}", f"y_bank{b}")
            cols = slice(CHUNK * b, CHUNK * (b + 1))
            for t in range(PACK):
                product(y_bank[:, t, :], w1_codes, w1_scales, t, offs_words[:, cols], offs_scales[:, cols])
            y_banks.append(y_bank)
        y = []
        for b in range(CHUNKS):
            y_chunk = sbuf.tile([P, PACK, CHUNK], F32, name=f"y{b}")
            nc.scalar.copy(flat(y_chunk), flat(y_banks[b]))
            y.append(y_chunk)

        q1 = {}
        q2 = sbuf.tile([P, CHUNKS, N], F32, name="q2")
        diff = sbuf.tile([P, CHUNKS, N], F32, name="diff")
        tanh = sbuf.tile([P, CHUNKS, N], F32, name="tanh", tag="tanh")
        abs_tanh = {}

        def squared_distances(i, first, count, tag, parts):
            looked_up = sbuf.tile([P, PACK, count * CHUNK], F32, name=f"c{i + 1}_{first}", tag=tag, align_bytes=64)
            entries = k_sb[i][:, LIST_COLS * first : LIST_COLS * (first + count)]
            d_banks = []
            for bank_tag, b, tiles, dst in parts:
                d_bank = bank(bank_tag, f"d_bank_{bank_tag}")
                for t in tiles:
                    nc.tensor.matmul(
                        d_bank[:, t, :], y[b][:, t, :], ident[:], start=(t == tiles[0]), stop=False, is_transpose=True
                    )
                d_banks.append(d_bank)
            for t in range(PACK):
                nc.vector.tensor_copy(looked_up[:, t, :], neg_c[t][:].indirect(entries))
                for d_bank, (bank_tag, b, tiles, dst) in zip(d_banks, parts):
                    if t in tiles:
                        block = looked_up[:, t, CHUNK * (b - first) : CHUNK * (b - first + 1)]
                        nc.tensor.matmul(
                            d_bank[:, t, :], block, ident[:], start=False, stop=(t == tiles[-1]), is_transpose=True
                        )
            for d_bank, (bank_tag, b, tiles, dst) in zip(d_banks, parts):
                cols = slice(P * tiles[0], P * (tiles[-1] + 1))
                nc.scalar.activation(dst[:, cols], flat(d_bank)[:, cols], ACT.Square, scale=math.sqrt(0.125))

        def first_component(first, count, tag):
            for b in range(first, first + count):
                q1[b] = sbuf.tile([P, N], F32, name=f"q1_{b}", tag=f"q1_{b}", align_bytes=64)
            parts = [(f"a{b % 2}", b, range(PACK), q1[b][:]) for b in range(first, first + count)]
            squared_distances(0, first, count, tag, parts)

        def second_component(first, count, tag):
            parts = [(f"a{2 + b % 2}", b, range(PACK), q2[:, b, :]) for b in range(first, first + count)]
            squared_distances(1, first, count, tag, parts)

        def difference_and_tanh(b, cols):
            nc.vector.scalar_tensor_tensor(
                diff[:, b, cols], q1[b][:, cols], log_pi[:, b : b + 1], q2[:, b, cols], ALU.subtract, ALU.subtract
            )
            nc.scalar.activation(tanh[:, b, cols], diff[:, b, cols], ACT.Tanh, scale=0.5, bias=half_l2[:, b : b + 1])

        def early_chunk_tanh(b):
            difference_and_tanh(b, slice(0, N))
            abs_tanh[b] = sbuf.tile([P, N], F32, name=f"abs_tanh{b}")[:]
            nc.scalar.activation(abs_tanh[b], tanh[:, b, :], ACT.Abs)

        def turn_back(src, tag, name):
            dst = bank(tag, name)
            for t in range(PACK):
                nc.tensor.transpose(dst[:, t, :], src[:, P * t : P * (t + 1)], ident[:])
            return dst

        min_banks = {}

        def minimum(b, dst):
            nc.vector.scalar_tensor_tensor(dst, diff[:, b, :], neg_l2[:, b : b + 1], q2[:, b, :], ALU.min, ALU.add)
            min_banks[b] = turn_back(dst, f"b{b}", f"min_bank{b}")

        first_component(0, 2, "pair")
        second_component(0, 2, "offs_words")
        early_chunk_tanh(0)
        first_component(2, 2, "pair")
        early_chunk_tanh(1)
        second_component(2, 1, "q1_0")
        halves = [("a3", LAST, range(0, 2), q2[:, LAST, :]), ("a0", LAST, range(2, 4), q2[:, LAST, :])]
        squared_distances(1, LAST, 1, "q1_1", halves)
        minimum(0, sbuf.tile([P, N], F32, name="min0", tag="q1_0", align_bytes=64)[:])
        difference_and_tanh(2, slice(0, N))
        for h in range(2):
            difference_and_tanh(LAST, slice(N // 2 * h, N // 2 * (h + 1)))

        after_last = sbuf.tile([P, 3, N], F32, name="after_last", tag=f"q1_{LAST}", align_bytes=64)
        tanh_banks = [turn_back(abs_tanh[b], f"a{b}", f"tanh_bank{b}") for b in range(SCALAR_CHUNKS)]
        minimum(1, after_last[:, 0, :])
        for b in range(SCALAR_CHUNKS, CHUNKS):
            magnitude = after_last[:, b - 1, :]
            nc.vector.scalar_tensor_tensor(magnitude, tanh[:, b, :], -1.0, tanh[:, b, :], ALU.mult, ALU.max)
            tanh_banks.append(turn_back(magnitude, f"a{b}", f"tanh_bank{b}"))
        last_mins = sbuf.tile([P, 2, N], F32, name="last_mins", tag="tanh")
        for b in range(2, CHUNKS):
            minimum(b, last_mins[:, b - 2, :])

        logs = sbuf.tile([P, CHUNKS, N], F32, name="logs", tag="half_l2")
        for b in range(CHUNKS):
            nc.scalar.activation(logs[:, b, :], flat(tanh_banks[b]), ACT.Ln, bias=1.0)
        out_rows = out_0.rearrange("(p t) j -> p t j", t=PACK)
        results = []
        for b in range(CHUNKS):
            result = sbuf.tile([P, PACK, CHUNK], F32, name=f"result{b}")
            nc.vector.scalar_tensor_tensor(flat(result), flat(min_banks[b]), -1.0, logs[:, b, :], ALU.mult, ALU.subtract)
            nc.sync.dma_start(out_rows[:, :, CHUNK * b : CHUNK * (b + 1)], result[:])
            results.append(result)
        rounded_out = []
        for b in range(CHUNKS):
            rounded = sbuf.tile([P, CHUNK, PACK], BF16, name=f"rounded_out{b}", align_bytes=64)
            copy = nc.scalar.copy if b < SCALAR_CHUNKS else nc.vector.tensor_copy
            copy(rounded[:], results[b][:].rearrange("p t j -> p j t"))
            rounded_out.append(rounded)
        out_codes = sbuf.tile([P, S], U32, name="out_codes", align_bytes=64)
        out_scales = sbuf.tile([P, S], U8, name="out_scales", align_bytes=64)
        out_words = out_1[0].rearrange("p n r -> p (n r)").bitcast(I32)
        for half in range(2):
            for b in (2 * half, 2 * half + 1):
                cols = slice(CHUNK * b, CHUNK * (b + 1))
                nc.vector.quantize_mx(
                    out=out_codes[:, cols].bitcast(FP8X4),
                    scales=out_scales[:, cols],
                    in_=rounded_out[b][:].rearrange("p j t -> p (j t)"),
                )
            cols = slice(S // 2 * half, S // 2 * (half + 1))
            nc.sync.dma_start(out_words[:, cols], out_codes[:, cols].bitcast(I32))
        for q in range(QUADS):
            queue = nc.scalar if q % 2 == 0 else nc.sync
            queue.dma_start(
                out_2[0, 4 * q : 4 * q + 4, :].bitcast(I32), out_scales[32 * q : 32 * q + 4, :].bitcast(I32)
            )
